import numpy as np, ml_dtypes
CORES = [3,7,11,15,131,135,139,143]
N = 8
import mx_ref
NC = 128
BF = ml_dtypes.bfloat16
def cut(t, i, w=512):
    return t[:, w * i:w * i + w]
def term(a, B):
    return np.stack([mx_ref.matmul(mx_ref.quantize(cut(a, i)), B) for i in range(4)], axis=2).reshape(128, -1)
def setup_inputs(rng):
    def f(*shape):
        return mx_ref.flush((rng.standard_normal(shape, dtype=np.float32) * np.exp2(rng.integers(-2, 3, shape[:-1] + (1,)))).astype(BF))
    return {"a": f(N, 128, 4 * 512), "b": f(N, 128, N * 4 * NC)}
def setup_inputs_blocks(rng):
    d = setup_inputs(rng)
    for k in ("a", "b"): d[k] = mx_ref.spread(d[k], rng, 2)
    return d
def setup_inputs_wide(rng):
    d = setup_inputs(rng)
    for k in ("a", "b"): d[k] = mx_ref.flush((d[k].astype(np.float32) * np.exp2(rng.integers(-4, 5, (N, 1, 1))).astype(np.float32)).astype(BF))
    return d
def setup_inputs_lossless(rng):
    a = np.zeros((N, 128, 4 * 128, 4), np.float32)
    for r in range(N):
        k = rng.integers(0, 512, size=4 * 128)
        a[r, k // 4, np.arange(4 * 128), k % 4] = 1.0
    size = np.repeat(2.0 ** rng.integers(-4, 5, size=(1, 1, (N * 4 * NC) // 4)), 4, axis=2)
    b = rng.integers(-1, 2, size=(N, 128, N * 4 * NC)) * size
    return {"a": a.reshape(N, 128, 4 * 512).astype(BF), "b": b.astype(np.float32).astype(BF)}
def reference(a, b):
    y = np.zeros((N, 128, 4 * NC), np.float32)
    for c in range(N):
        y[c] = mx_ref.total([term(a[r], mx_ref.quantize(cut(b[r], c, 4 * NC))) for r in range(N)])
    return {"y": y}

@@ -1,0 +1,259 @@
+from concourse.bass import DstId, RemoteDMATransfer
+from concourse.mybir import dt, AluOpType, ActivationFunctionType
+
+N = 8
+TW = 128
+TE = 4 * TW
+NP = N - 1
+ROT = 7
+PAIRED = True
+
+SCRATCH = {
+    "abf": ("sbuf", [128, 4 * TE], "bfloat16"),
+    "bbf": ("sbuf", [128, N * TE], "bfloat16"),
+    "aq": ("sbuf", [128, 4 * TW], "float8_e4m3fn_x4"),
+    "asc": ("sbuf", [128, 4 * TW], "uint8"),
+    "bq": ("sbuf", [128, N * TW], "float8_e4m3fn_x4"),
+    "bsc": ("sbuf", [128, N * TW], "uint8"),
+    "iot": ("sbuf", [128, 128], "float32"),
+    "ubf": ("sbuf", [128, 4 * TE], "bfloat16"),
+    "uq": ("sbuf", [128, TE], "float8_e4m3fn_x4"),
+    "usc": ("sbuf", [128, TE], "uint8"),
+    "h": ("sbuf", [128, NP * TE], "bfloat16"),
+    "hq": ("sbuf", [128, NP * TW], "float8_e4m3fn_x4"),
+    "hsc": ("sbuf", [128, NP * TW], "uint8"),
+    "lq": ("sbuf", [128, NP * TW], "float8_e4m3fn_x4"),
+    "lsc": ("sbuf", [128, NP * TW], "uint8"),
+    "own": ("sbuf", [128, TE], "float32"),
+    "ysb": ("sbuf", [128, TE], "float32"),
+    "ps": ("psum", [128, 512 * (ROT + 1)], "float32"),
+}
+SEMAPHORES = (
+    ["ldA0", "ldA1", "ix", "ms", "eq", "qU", "qA0", "qA1", "co", "snt", "dec", "y0", "y1", "st0", "st1"]
+    + ["ldB%d" % i for i in range(4)] + ["qB%d" % i for i in range(4)] + ["mo%d" % i for i in range(4)]
+    + [p + "%d" % k for k in range(NP) for p in ("ml", "mh", "cl", "ch", "cv", "qz", "arr")]
+)
+
+
+def _far(topo, a, b):
+    if topo.host(a) == topo.host(b) and topo.chip(a) == topo.chip(b):
+        return 0
+    if topo.mates(a, b):
+        return 1
+    if topo.same_plane(a, b):
+        return 2
+    return 3
+
+
+def _order(topo, cores, me):
+    return sorted([c for c in cores if c != me], key=lambda c: (-_far(topo, me, c), topo.die(c) != topo.die(me), c))
+
+
+def _bits(m):
+    return [e for e in range(m.bit_length()) if (m >> e) & 1]
+
+
+def _mask(es):
+    m = 0
+    for e in es:
+        m |= 1 << e
+    return m
+
+
+def _plan(topo, cores, me):
+    peers = _order(topo, cores, me)
+    common = topo.mask(me, peers[0])
+    for c in peers:
+        common &= topo.mask(me, c)
+    cb = _bits(common)
+    masks = []
+    for k, c in enumerate(peers):
+        if _far(topo, me, c) == 0:
+            masks.append(_mask([e for e in _bits(topo.mask(me, c)) if e not in cb] or cb))
+        elif PAIRED:
+            masks.append(_mask(cb[:len(cb) // 2] if k % 2 == 0 else cb[len(cb) // 2:]))
+        else:
+            masks.append(common)
+    return peers, masks
+
+
+def _runs(rs):
+    out = []
+    for r in sorted(rs):
+        if out and out[-1][1] == r:
+            out[-1][1] = r + 1
+        else:
+            out.append([r, r + 1])
+    return out
+
+
+def rank_program(g, core, T, topo):
+    rank = T.rank_of(core)
+    if rank is None:
+        return
+    cores = list(T.cores)
+    sem = T.sem
+    sy, sc, ve, te = g.sync, g.scalar, g.vector, g.tensor
+    peers, masks = _plan(topo, cores, core)
+    pr = [T.rank_of(c) for c in peers]
+    groups = [_runs(pr[0:2]), _runs(pr[2:4]), _runs(pr[4:6]), _runs([pr[6], rank])]
+    half = 2 * TE
+
+    def load_a(q, hf):
+        q.dma_start(T.abf[:, half * hf:half * (hf + 1)], T.a[:, half * hf:half * (hf + 1)]).then_inc(sem["ldA%d" % hf], 16)
+
+    def load_b(q, gi):
+        for lo, hi in groups[gi]:
+            q.dma_start(T.bbf[:, TE * lo:TE * hi], T.b[:, TE * lo:TE * hi]).then_inc(sem["ldB%d" % gi], 16)
+
+    load_a(sy, 0)
+    load_b(sc, 0)
+    load_a(sy, 1)
+    load_b(sc, 1)
+    load_b(sy, 2)
+    load_b(sc, 3)
+
+    g.iota(T.iot[:], [[-1, 128]], 0, 1, allow_small_or_imprecise_dtypes=True).then_inc(sem.ix, 1)
+    ve.memset(T.ubf[:], 0.0).then_inc(sem.ms, 1)
+    ve.wait_ge(sem.ms, 1)
+    ve.wait_ge(sem.ix, 1)
+    for t in range(4):
+        ve.tensor_scalar(T.ubf[:, 5 * t:4 * TE:16], T.iot[:], 0.0, None, AluOpType.is_equal).then_inc(sem.eq, 1)
+    ve.wait_ge(sem.eq, 4)
+    ve.quantize_mx(T.uq[:], T.usc[:], T.ubf[:]).then_inc(sem.qU, 1)
+
+    seq = [(0, 0), (1, 0), (0, 1), (1, 1)] + [(k, hf) for k in range(2, NP) for hf in (0, 1)]
+    seen = set()
+
+    def tw(name, val):
+        if (name, val) not in seen:
+            seen.add((name, val))
+            te.wait_ge(sem[name], val)
+
+    free, bank = [], {}
+    for a, (k, hf) in enumerate(seq):
+        tw("qA%d" % hf, 1)
+        tw("qB%d" % (k // 2), len(groups[k // 2]))
+        if a >= ROT:
+            tw(*free[a - ROT])
+        c, base = pr[k], 512 * (a % ROT)
+        te.matmul_mx(T.ps[:, base:base + 2 * TW], T.bq[:, TW * c:TW * (c + 1)], T.bsc[:, TW * c:TW * (c + 1)],
+                     T.aq[:, 2 * TW * hf:2 * TW * (hf + 1)], T.asc[:, 2 * TW * hf:2 * TW * (hf + 1)],
+                     True, True).then_inc(sem[("mh%d" if hf else "ml%d") % k], 1)
+        free.append(("ch%d" % k, 1) if hf else ("cl%d" % k, 2))
+        bank[(k, hf)] = base
+    obank = []
+    for i in range(4):
+        a = len(seq) + i
+        tw(*free[a - ROT])
+        base = 512 * (a % ROT)
+        te.matmul_mx(T.ps[:, base:base + TW], T.aq[:, TW * i:TW * (i + 1)], T.asc[:, TW * i:TW * (i + 1)],
+                     T.bq[:, TW * rank:TW * (rank + 1)], T.bsc[:, TW * rank:TW * (rank + 1)],
+                     True, True).then_inc(sem["mo%d" % i], 1)
+        obank.append(base)
+    acc = 512 * ROT
+    tw("qU", 1)
+    for s in range(NP):
+        sp, sm = _plan(topo, cores, peers[s])
+        te.wait_ge(sem["arr%d" % s], 2 * len(_bits(sm[sp.index(core)])))
+        mm = te.matmul_mx(T.ps[:, acc:acc + TE], T.lq[:, TW * s:TW * (s + 1)], T.lsc[:, TW * s:TW * (s + 1)],
+                          T.uq[:], T.usc[:], s == 0, s == NP - 1)
+        if s == NP - 1:
+            mm.then_inc(sem.dec, 1)
+
+    def s_lo(k):
+        sc.wait_ge(sem["ml%d" % k], 1)
+        for i in (0, 1):
+            sc.activation(T.h[:, TE * k + i:TE * (k + 1):4], T.ps[:, bank[(k, 0)] + TW * i:bank[(k, 0)] + TW * (i + 1)],
+                          ActivationFunctionType.Copy).then_inc(sem["cl%d" % k], 1)
+
+    def s_hi(k):
+        sc.wait_ge(sem["mh%d" % k], 1)
+        sc.wait_ge(sem["cv%d" % k], 1)
+        sc.activation(T.h[:, TE * k + 2:TE * (k + 1):4], T.ps[:, bank[(k, 1)]:bank[(k, 1)] + TW],
+                      ActivationFunctionType.Copy).then_inc(sem["ch%d" % k], 1)
+
+    s_lo(0)
+    s_lo(1)
+    s_hi(0)
+    s_hi(1)
+    for k in range(2, NP):
+        s_lo(k)
+        s_hi(k)
+    for i in range(4):
+        sc.wait_ge(sem["mo%d" % i], 1)
+        sc.activation(T.own[:, i:TE:4], T.ps[:, obank[i]:obank[i] + TW], ActivationFunctionType.Copy).then_inc(sem.co, 1)
+
+    def q_a(hf):
+        ve.wait_ge(sem["ldA%d" % hf], 16)
+        ve.quantize_mx(T.aq[:, 2 * TW * hf:2 * TW * (hf + 1)], T.asc[:, 2 * TW * hf:2 * TW * (hf + 1)],
+                       T.abf[:, half * hf:half * (hf + 1)]).then_inc(sem["qA%d" % hf], 1)
+
+    def q_b(gi):
+        ve.wait_ge(sem["ldB%d" % gi], 16 * len(groups[gi]))
+        for lo, hi in groups[gi]:
+            ve.quantize_mx(T.bq[:, TW * lo:TW * hi], T.bsc[:, TW * lo:TW * hi],
+                           T.bbf[:, TE * lo:TE * hi]).then_inc(sem["qB%d" % gi], 1)
+
+    def v_cp(k):
+        ve.wait_ge(sem["mh%d" % k], 1)
+        ve.tensor_copy(T.h[:, TE * k + 3:TE * (k + 1):4],
+                       T.ps[:, bank[(k, 1)] + TW:bank[(k, 1)] + 2 * TW]).then_inc(sem["cv%d" % k], 1)
+
+    def v_q(k):
+        ve.wait_ge(sem["cv%d" % k], 1)
+        ve.wait_ge(sem["cl%d" % k], 2)
+        ve.wait_ge(sem["ch%d" % k], 1)
+        ve.quantize_mx(T.hq[:, TW * k:TW * (k + 1)], T.hsc[:, TW * k:TW * (k + 1)],
+                       T.h[:, TE * k:TE * (k + 1)]).then_inc(sem["qz%d" % k], 1)
+
+    q_a(0)
+    q_b(0)
+    q_a(1)
+    for gi in range(3):
+        v_cp(2 * gi)
+        q_b(gi + 1)
+        v_q(2 * gi)
+        v_cp(2 * gi + 1)
+        v_q(2 * gi + 1)
+    v_cp(NP - 1)
+    v_q(NP - 1)
+
+    sent = 0
+    batches = [[0, 1], [2, 3], [4, 5], [6]] if PAIRED else [[k] for k in range(NP)]
+    for batch in batches:
+        for k in batch:
+            g.wait_ge(sem["qz%d" % k], 1)
+        for codes in (True, False):
+            trs = []
+            for k in batch:
+                rid, pid = topo.addr(peers[k], core)
+                s = _order(topo, cores, peers[k]).index(core)
+                if codes:
+                    src = T.hq[:, TW * k:TW * (k + 1)].bitcast(dt.uint8)
+                    dst = T.lq[:, TW * s:TW * (s + 1)].bitcast(dt.uint8)
+                else:
+                    src = T.hsc[:, TW * k:TW * (k + 1)]
+                    dst = T.lsc[:, TW * s:TW * (s + 1)]
+                trs.append((dst, src, sem["arr%d" % s], pid, rid, masks[k]))
+                sent += len(_bits(masks[k]))
+            if len(trs) == 1:
+                dst, src, rs, pid, rid, m = trs[0]
+                g.remote_dma(dst, src, rs, sem.snt, pid, rid, m)
+            else:
+                g.remote_dma_fused([RemoteDMATransfer(dst_ids=[DstId(rid=rid, pnc=pid)], dma_engine_mask=m,
+                                                      remote_sem=rs, src=src, dst=dst)
+                                    for dst, src, rs, pid, rid, m in trs], local_sem=sem.snt)
+    g.wait_ge(sem.snt, sent)
+
+    hw = TE // 2
+    ve.wait_ge(sem.co, 4)
+    ve.wait_ge(sem.dec, 1)
+    ve.tensor_tensor(T.ysb[:, 0:hw], T.ps[:, acc:acc + hw], T.own[:, 0:hw], AluOpType.add).then_inc(sem.y0, 1)
+    ve.tensor_tensor(T.ysb[:, hw:TE], T.ps[:, acc + hw:acc + TE], T.own[:, hw:TE], AluOpType.add).then_inc(sem.y1, 1)
+    sy.wait_ge(sem.y0, 1)
+    sy.dma_start(T.y[:, 0:hw], T.ysb[:, 0:hw]).then_inc(sem.st0, 16)
+    sc.wait_ge(sem.y1, 1)
+    sc.dma_start(T.y[:, hw:TE], T.ysb[:, hw:TE]).then_inc(sem.st1, 16)
+    sy.wait_ge(sem.st0, 16)
+    sc.wait_ge(sem.st1, 16)

@@ -1,4 +1,3 @@
-from concourse.bass import DstId, RemoteDMATransfer
 from concourse.mybir import dt, AluOpType, ActivationFunctionType
 
 N = 8
@@ -6,7 +5,7 @@ TW = 128
 TE = 4 * TW
 NP = N - 1
 ROT = 7
-PAIRED = True
+LATE = 2
 
 SCRATCH = {
     "abf": ("sbuf", [128, 4 * TE], "bfloat16"),
@@ -29,24 +28,25 @@ SCRATCH = {
     "ps": ("psum", [128, 512 * (ROT + 1)], "float32"),
 }
 SEMAPHORES = (
-    ["ldA0", "ldA1", "ix", "ms", "eq", "qU", "qA0", "qA1", "co", "snt", "dec", "y0", "y1", "st0", "st1"]
-    + ["ldB%d" % i for i in range(4)] + ["qB%d" % i for i in range(4)] + ["mo%d" % i for i in range(4)]
+    ["ldA0", "ldA1", "ix", "ms", "eq", "qU", "qA0", "qA1", "co", "snt", "dec", "pm", "y0", "y1", "st0", "st1"]
+    + ["ldB%d" % i for i in range(4)] + ["qB%d" % i for i in range(6)]
+    + ["mo%d" % i for i in range(4)] + ["dl%d" % i for i in range(4)]
     + [p + "%d" % k for k in range(NP) for p in ("ml", "mh", "cl", "ch", "cv", "qz", "arr")]
 )
 
 
-def _far(topo, a, b):
+def _turn(topo, a, b):
     if topo.host(a) == topo.host(b) and topo.chip(a) == topo.chip(b):
-        return 0
-    if topo.mates(a, b):
-        return 1
-    if topo.same_plane(a, b):
         return 2
-    return 3
+    if topo.mates(a, b):
+        return 3
+    if topo.same_plane(a, b):
+        return 1
+    return 0
 
 
 def _order(topo, cores, me):
-    return sorted([c for c in cores if c != me], key=lambda c: (-_far(topo, me, c), topo.die(c) != topo.die(me), c))
+    return sorted([c for c in cores if c != me], key=lambda c: (_turn(topo, me, c), topo.die(c) != topo.die(me), c))
 
 
 def _bits(m):
@@ -67,13 +67,9 @@ def _plan(topo, cores, me):
         common &= topo.mask(me, c)
     cb = _bits(common)
     masks = []
-    for k, c in enumerate(peers):
-        if _far(topo, me, c) == 0:
-            masks.append(_mask([e for e in _bits(topo.mask(me, c)) if e not in cb] or cb))
-        elif PAIRED:
-            masks.append(_mask(cb[:len(cb) // 2] if k % 2 == 0 else cb[len(cb) // 2:]))
-        else:
-            masks.append(common)
+    for c in peers:
+        rest = [e for e in _bits(topo.mask(me, c)) if e not in cb]
+        masks.append(_mask(rest) if rest else common)
     return peers, masks
 
 
@@ -94,17 +90,21 @@ def rank_program(g, core, T, topo):
     cores = list(T.cores)
     sem = T.sem
     sy, sc, ve, te = g.sync, g.scalar, g.vector, g.tensor
+    Copy = ActivationFunctionType.Copy
     peers, masks = _plan(topo, cores, core)
     pr = [T.rank_of(c) for c in peers]
-    groups = [_runs(pr[0:2]), _runs(pr[2:4]), _runs(pr[4:6]), _runs([pr[6], rank])]
+    lunits = [_runs(pr[0:2]), _runs(pr[2:4]), _runs([pr[4], rank]), _runs(pr[5:7])]
+    qunits = [(_runs(pr[0:1]), 0), (_runs(pr[1:2]), 0), (_runs(pr[2:4]), 1), (_runs(pr[4:5]), 2),
+              (_runs(pr[5:7]), 3), (_runs([rank]), 2)]
+    unit_of = [0, 1, 2, 2, 3, 4, 4]
     half = 2 * TE
 
     def load_a(q, hf):
         q.dma_start(T.abf[:, half * hf:half * (hf + 1)], T.a[:, half * hf:half * (hf + 1)]).then_inc(sem["ldA%d" % hf], 16)
 
-    def load_b(q, gi):
-        for lo, hi in groups[gi]:
-            q.dma_start(T.bbf[:, TE * lo:TE * hi], T.b[:, TE * lo:TE * hi]).then_inc(sem["ldB%d" % gi], 16)
+    def load_b(q, u):
+        for lo, hi in lunits[u]:
+            q.dma_start(T.bbf[:, TE * lo:TE * hi], T.b[:, TE * lo:TE * hi]).then_inc(sem["ldB%d" % u], 16)
 
     load_a(sy, 0)
     load_b(sc, 0)
@@ -122,7 +122,7 @@ def rank_program(g, core, T, topo):
     ve.wait_ge(sem.eq, 4)
     ve.quantize_mx(T.uq[:], T.usc[:], T.ubf[:]).then_inc(sem.qU, 1)
 
-    seq = [(0, 0), (1, 0), (0, 1), (1, 1)] + [(k, hf) for k in range(2, NP) for hf in (0, 1)]
+    seq = [(k, hf) for k in range(NP) for hf in (0, 1)]
     seen = set()
 
     def tw(name, val):
@@ -132,128 +132,126 @@ def rank_program(g, core, T, topo):
 
     free, bank = [], {}
     for a, (k, hf) in enumerate(seq):
+        tw("qB%d" % unit_of[k], len(qunits[unit_of[k]][0]))
         tw("qA%d" % hf, 1)
-        tw("qB%d" % (k // 2), len(groups[k // 2]))
         if a >= ROT:
             tw(*free[a - ROT])
         c, base = pr[k], 512 * (a % ROT)
         te.matmul_mx(T.ps[:, base:base + 2 * TW], T.bq[:, TW * c:TW * (c + 1)], T.bsc[:, TW * c:TW * (c + 1)],
                      T.aq[:, 2 * TW * hf:2 * TW * (hf + 1)], T.asc[:, 2 * TW * hf:2 * TW * (hf + 1)],
                      True, True).then_inc(sem[("mh%d" if hf else "ml%d") % k], 1)
-        free.append(("ch%d" % k, 1) if hf else ("cl%d" % k, 2))
+        free.append(("cv%d" % k, 1) if hf else ("cl%d" % k, 2))
         bank[(k, hf)] = base
     obank = []
+    tw("qB5", len(qunits[5][0]))
     for i in range(4):
-        a = len(seq) + i
+        a = len(free)
         tw(*free[a - ROT])
         base = 512 * (a % ROT)
         te.matmul_mx(T.ps[:, base:base + TW], T.aq[:, TW * i:TW * (i + 1)], T.asc[:, TW * i:TW * (i + 1)],
                      T.bq[:, TW * rank:TW * (rank + 1)], T.bsc[:, TW * rank:TW * (rank + 1)],
                      True, True).then_inc(sem["mo%d" % i], 1)
+        free.append(("co", 4))
         obank.append(base)
     acc = 512 * ROT
+    early = NP - LATE
     tw("qU", 1)
+    lbank = []
+    for q in range(4):
+        a = len(free)
+        lbank.append((512 * (a % ROT), free[a - ROT]))
+        free.append(None)
     for s in range(NP):
         sp, sm = _plan(topo, cores, peers[s])
         te.wait_ge(sem["arr%d" % s], 2 * len(_bits(sm[sp.index(core)])))
-        mm = te.matmul_mx(T.ps[:, acc:acc + TE], T.lq[:, TW * s:TW * (s + 1)], T.lsc[:, TW * s:TW * (s + 1)],
-                          T.uq[:], T.usc[:], s == 0, s == NP - 1)
-        if s == NP - 1:
-            mm.then_inc(sem.dec, 1)
+        if s < early:
+            mm = te.matmul_mx(T.ps[:, acc:acc + TE], T.lq[:, TW * s:TW * (s + 1)], T.lsc[:, TW * s:TW * (s + 1)],
+                              T.uq[:], T.usc[:], s == 0, s == early - 1)
+            if s == early - 1:
+                mm.then_inc(sem.dec, 1)
+        else:
+            for q in range(4):
+                base, fr = lbank[q]
+                tw(*fr)
+                mm = te.matmul_mx(T.ps[:, base:base + TW], T.lq[:, TW * s:TW * (s + 1)], T.lsc[:, TW * s:TW * (s + 1)],
+                                  T.uq[:, TW * q:TW * (q + 1)], T.usc[:, TW * q:TW * (q + 1)], s == early, s == NP - 1)
+                if s == NP - 1:
+                    mm.then_inc(sem["dl%d" % q], 1)
 
-    def s_lo(k):
+    for k in range(NP):
         sc.wait_ge(sem["ml%d" % k], 1)
         for i in (0, 1):
             sc.activation(T.h[:, TE * k + i:TE * (k + 1):4], T.ps[:, bank[(k, 0)] + TW * i:bank[(k, 0)] + TW * (i + 1)],
-                          ActivationFunctionType.Copy).then_inc(sem["cl%d" % k], 1)
-
-    def s_hi(k):
+                          Copy).then_inc(sem["cl%d" % k], 1)
         sc.wait_ge(sem["mh%d" % k], 1)
-        sc.wait_ge(sem["cv%d" % k], 1)
         sc.activation(T.h[:, TE * k + 2:TE * (k + 1):4], T.ps[:, bank[(k, 1)]:bank[(k, 1)] + TW],
-                      ActivationFunctionType.Copy).then_inc(sem["ch%d" % k], 1)
-
-    s_lo(0)
-    s_lo(1)
-    s_hi(0)
-    s_hi(1)
-    for k in range(2, NP):
-        s_lo(k)
-        s_hi(k)
+                      Copy).then_inc(sem["ch%d" % k], 1)
     for i in range(4):
         sc.wait_ge(sem["mo%d" % i], 1)
-        sc.activation(T.own[:, i:TE:4], T.ps[:, obank[i]:obank[i] + TW], ActivationFunctionType.Copy).then_inc(sem.co, 1)
+        sc.activation(T.own[:, i:TE:4], T.ps[:, obank[i]:obank[i] + TW], Copy).then_inc(sem.co, 1)
 
     def q_a(hf):
         ve.wait_ge(sem["ldA%d" % hf], 16)
         ve.quantize_mx(T.aq[:, 2 * TW * hf:2 * TW * (hf + 1)], T.asc[:, 2 * TW * hf:2 * TW * (hf + 1)],
                        T.abf[:, half * hf:half * (hf + 1)]).then_inc(sem["qA%d" % hf], 1)
 
-    def q_b(gi):
-        ve.wait_ge(sem["ldB%d" % gi], 16 * len(groups[gi]))
-        for lo, hi in groups[gi]:
+    def q_b(u):
+        runs, lu = qunits[u]
+        ve.wait_ge(sem["ldB%d" % lu], 16 * len(lunits[lu]))
+        for lo, hi in runs:
             ve.quantize_mx(T.bq[:, TW * lo:TW * hi], T.bsc[:, TW * lo:TW * hi],
-                           T.bbf[:, TE * lo:TE * hi]).then_inc(sem["qB%d" % gi], 1)
+                           T.bbf[:, TE * lo:TE * hi]).then_inc(sem["qB%d" % u], 1)
 
-    def v_cp(k):
+    def tile(k):
         ve.wait_ge(sem["mh%d" % k], 1)
-        ve.tensor_copy(T.h[:, TE * k + 3:TE * (k + 1):4],
-                       T.ps[:, bank[(k, 1)] + TW:bank[(k, 1)] + 2 * TW]).then_inc(sem["cv%d" % k], 1)
-
-    def v_q(k):
-        ve.wait_ge(sem["cv%d" % k], 1)
         ve.wait_ge(sem["cl%d" % k], 2)
         ve.wait_ge(sem["ch%d" % k], 1)
+        ve.tensor_copy(T.h[:, TE * k + 3:TE * (k + 1):4],
+                       T.ps[:, bank[(k, 1)] + TW:bank[(k, 1)] + 2 * TW]).then_inc(sem["cv%d" % k], 1)
+        ve.wait_ge(sem["cv%d" % k], 1)
         ve.quantize_mx(T.hq[:, TW * k:TW * (k + 1)], T.hsc[:, TW * k:TW * (k + 1)],
                        T.h[:, TE * k:TE * (k + 1)]).then_inc(sem["qz%d" % k], 1)
 
     q_a(0)
     q_b(0)
     q_a(1)
-    for gi in range(3):
-        v_cp(2 * gi)
-        q_b(gi + 1)
-        v_q(2 * gi)
-        v_cp(2 * gi + 1)
-        v_q(2 * gi + 1)
-    v_cp(NP - 1)
-    v_q(NP - 1)
+    q_b(1)
+    q_b(2)
+    tile(0)
+    tile(1)
+    q_b(3)
+    tile(2)
+    q_b(4)
+    tile(3)
+    tile(4)
+    q_b(5)
+    tile(5)
+    tile(6)
 
     sent = 0
-    batches = [[0, 1], [2, 3], [4, 5], [6]] if PAIRED else [[k] for k in range(NP)]
-    for batch in batches:
-        for k in batch:
-            g.wait_ge(sem["qz%d" % k], 1)
-        for codes in (True, False):
-            trs = []
-            for k in batch:
-                rid, pid = topo.addr(peers[k], core)
-                s = _order(topo, cores, peers[k]).index(core)
-                if codes:
-                    src = T.hq[:, TW * k:TW * (k + 1)].bitcast(dt.uint8)
-                    dst = T.lq[:, TW * s:TW * (s + 1)].bitcast(dt.uint8)
-                else:
-                    src = T.hsc[:, TW * k:TW * (k + 1)]
-                    dst = T.lsc[:, TW * s:TW * (s + 1)]
-                trs.append((dst, src, sem["arr%d" % s], pid, rid, masks[k]))
-                sent += len(_bits(masks[k]))
-            if len(trs) == 1:
-                dst, src, rs, pid, rid, m = trs[0]
-                g.remote_dma(dst, src, rs, sem.snt, pid, rid, m)
-            else:
-                g.remote_dma_fused([RemoteDMATransfer(dst_ids=[DstId(rid=rid, pnc=pid)], dma_engine_mask=m,
-                                                      remote_sem=rs, src=src, dst=dst)
-                                    for dst, src, rs, pid, rid, m in trs], local_sem=sem.snt)
+    for k in range(NP):
+        g.wait_ge(sem["qz%d" % k], 1)
+        rid, pid = topo.addr(peers[k], core)
+        s = _order(topo, cores, peers[k]).index(core)
+        g.remote_dma(T.lq[:, TW * s:TW * (s + 1)].bitcast(dt.uint8), T.hq[:, TW * k:TW * (k + 1)].bitcast(dt.uint8),
+                     sem["arr%d" % s], sem.snt, pid, rid, masks[k])
+        g.remote_dma(T.lsc[:, TW * s:TW * (s + 1)], T.hsc[:, TW * k:TW * (k + 1)],
+                     sem["arr%d" % s], sem.snt, pid, rid, masks[k])
+        sent += 2 * len(_bits(masks[k]))
     g.wait_ge(sem.snt, sent)
 
-    hw = TE // 2
     ve.wait_ge(sem.co, 4)
     ve.wait_ge(sem.dec, 1)
-    ve.tensor_tensor(T.ysb[:, 0:hw], T.ps[:, acc:acc + hw], T.own[:, 0:hw], AluOpType.add).then_inc(sem.y0, 1)
-    ve.tensor_tensor(T.ysb[:, hw:TE], T.ps[:, acc + hw:acc + TE], T.own[:, hw:TE], AluOpType.add).then_inc(sem.y1, 1)
-    sy.wait_ge(sem.y0, 1)
+    ve.tensor_tensor(T.own[:], T.ps[:, acc:acc + TE], T.own[:], AluOpType.add).then_inc(sem.pm, 1)
+    ve.wait_ge(sem.pm, 1)
+    for q in range(4):
+        ve.wait_ge(sem["dl%d" % q], 1)
+        ve.tensor_tensor(T.ysb[:, TW * q:TW * (q + 1)], T.ps[:, lbank[q][0]:lbank[q][0] + TW],
+                         T.own[:, TW * q:TW * (q + 1)], AluOpType.add).then_inc(sem["y%d" % (q // 2)], 1)
+    hw = TE // 2
+    sy.wait_ge(sem.y0, 2)
     sy.dma_start(T.y[:, 0:hw], T.ysb[:, 0:hw]).then_inc(sem.st0, 16)
-    sc.wait_ge(sem.y1, 1)
+    sc.wait_ge(sem.y1, 2)
     sc.dma_start(T.y[:, hw:TE], T.ysb[:, hw:TE]).then_inc(sem.st1, 16)
     sy.wait_ge(sem.st0, 16)
     sc.wait_ge(sem.st1, 16)

from concourse.mybir import dt, AluOpType, ActivationFunctionType

N = 8
TW = 128
TE = 4 * TW
NP = N - 1
ROT = 7
LATE = 2

SCRATCH = {
    "abf": ("sbuf", [128, 4 * TE], "bfloat16"),
    "bbf": ("sbuf", [128, N * TE], "bfloat16"),
    "aq": ("sbuf", [128, 4 * TW], "float8_e4m3fn_x4"),
    "asc": ("sbuf", [128, 4 * TW], "uint8"),
    "bq": ("sbuf", [128, N * TW], "float8_e4m3fn_x4"),
    "bsc": ("sbuf", [128, N * TW], "uint8"),
    "iot": ("sbuf", [128, 128], "float32"),
    "ubf": ("sbuf", [128, 4 * TE], "bfloat16"),
    "uq": ("sbuf", [128, TE], "float8_e4m3fn_x4"),
    "usc": ("sbuf", [128, TE], "uint8"),
    "h": ("sbuf", [128, NP * TE], "bfloat16"),
    "hq": ("sbuf", [128, NP * TW], "float8_e4m3fn_x4"),
    "hsc": ("sbuf", [128, NP * TW], "uint8"),
    "lq": ("sbuf", [128, NP * TW], "float8_e4m3fn_x4"),
    "lsc": ("sbuf", [128, NP * TW], "uint8"),
    "own": ("sbuf", [128, TE], "float32"),
    "ysb": ("sbuf", [128, TE], "float32"),
    "ps": ("psum", [128, 512 * (ROT + 1)], "float32"),
}
SEMAPHORES = (
    ["ldA0", "ldA1", "ix", "ms", "eq", "qU", "qA0", "qA1", "co", "snt", "dec", "pm", "y0", "y1", "st0", "st1"]
    + ["ldB%d" % i for i in range(4)] + ["qB%d" % i for i in range(6)]
    + ["mo%d" % i for i in range(4)] + ["dl%d" % i for i in range(4)]
    + [p + "%d" % k for k in range(NP) for p in ("ml", "mh", "cl", "ch", "cv", "qz", "arr")]
)


def _turn(topo, a, b):
    if topo.host(a) == topo.host(b) and topo.chip(a) == topo.chip(b):
        return 2
    if topo.mates(a, b):
        return 3
    if topo.same_plane(a, b):
        return 1
    return 0


def _order(topo, cores, me):
    return sorted([c for c in cores if c != me], key=lambda c: (_turn(topo, me, c), topo.die(c) != topo.die(me), c))


def _bits(m):
    return [e for e in range(m.bit_length()) if (m >> e) & 1]


def _mask(es):
    m = 0
    for e in es:
        m |= 1 << e
    return m


def _plan(topo, cores, me):
    peers = _order(topo, cores, me)
    common = topo.mask(me, peers[0])
    for c in peers:
        common &= topo.mask(me, c)
    cb = _bits(common)
    masks = []
    for c in peers:
        rest = [e for e in _bits(topo.mask(me, c)) if e not in cb]
        masks.append(_mask(rest) if rest else common)
    return peers, masks


def _runs(rs):
    out = []
    for r in sorted(rs):
        if out and out[-1][1] == r:
            out[-1][1] = r + 1
        else:
            out.append([r, r + 1])
    return out


def rank_program(g, core, T, topo):
    rank = T.rank_of(core)
    if rank is None:
        return
    cores = list(T.cores)
    sem = T.sem
    sy, sc, ve, te = g.sync, g.scalar, g.vector, g.tensor
    Copy = ActivationFunctionType.Copy
    peers, masks = _plan(topo, cores, core)
    pr = [T.rank_of(c) for c in peers]
    lunits = [_runs(pr[0:2]), _runs(pr[2:4]), _runs([pr[4], rank]), _runs(pr[5:7])]
    qunits = [(_runs(pr[0:1]), 0), (_runs(pr[1:2]), 0), (_runs(pr[2:4]), 1), (_runs(pr[4:5]), 2),
              (_runs(pr[5:7]), 3), (_runs([rank]), 2)]
    unit_of = [0, 1, 2, 2, 3, 4, 4]
    half = 2 * TE

    def load_a(q, hf):
        q.dma_start(T.abf[:, half * hf:half * (hf + 1)], T.a[:, half * hf:half * (hf + 1)]).then_inc(sem["ldA%d" % hf], 16)

    def load_b(q, u):
        for lo, hi in lunits[u]:
            q.dma_start(T.bbf[:, TE * lo:TE * hi], T.b[:, TE * lo:TE * hi]).then_inc(sem["ldB%d" % u], 16)

    load_a(sy, 0)
    load_b(sc, 0)
    load_a(sy, 1)
    load_b(sc, 1)
    load_b(sy, 2)
    load_b(sc, 3)

    g.iota(T.iot[:], [[-1, 128]], 0, 1, allow_small_or_imprecise_dtypes=True).then_inc(sem.ix, 1)
    ve.memset(T.ubf[:], 0.0).then_inc(sem.ms, 1)
    ve.wait_ge(sem.ms, 1)
    ve.wait_ge(sem.ix, 1)
    for t in range(4):
        ve.tensor_scalar(T.ubf[:, 5 * t:4 * TE:16], T.iot[:], 0.0, None, AluOpType.is_equal).then_inc(sem.eq, 1)
    ve.wait_ge(sem.eq, 4)
    ve.quantize_mx(T.uq[:], T.usc[:], T.ubf[:]).then_inc(sem.qU, 1)

    seq = [(k, hf) for k in range(NP) for hf in (0, 1)]
    seen = set()

    def tw(name, val):
        if (name, val) not in seen:
            seen.add((name, val))
            te.wait_ge(sem[name], val)

    free, bank = [], {}
    for a, (k, hf) in enumerate(seq):
        tw("qB%d" % unit_of[k], len(qunits[unit_of[k]][0]))
        tw("qA%d" % hf, 1)
        if a >= ROT:
            tw(*free[a - ROT])
        c, base = pr[k], 512 * (a % ROT)
        te.matmul_mx(T.ps[:, base:base + 2 * TW], T.bq[:, TW * c:TW * (c + 1)], T.bsc[:, TW * c:TW * (c + 1)],
                     T.aq[:, 2 * TW * hf:2 * TW * (hf + 1)], T.asc[:, 2 * TW * hf:2 * TW * (hf + 1)],
                     True, True).then_inc(sem[("mh%d" if hf else "ml%d") % k], 1)
        free.append(("cv%d" % k, 1) if hf else ("cl%d" % k, 2))
        bank[(k, hf)] = base
    obank = []
    tw("qB5", len(qunits[5][0]))
    for i in range(4):
        a = len(free)
        tw(*free[a - ROT])
        base = 512 * (a % ROT)
        te.matmul_mx(T.ps[:, base:base + TW], T.aq[:, TW * i:TW * (i + 1)], T.asc[:, TW * i:TW * (i + 1)],
                     T.bq[:, TW * rank:TW * (rank + 1)], T.bsc[:, TW * rank:TW * (rank + 1)],
                     True, True).then_inc(sem["mo%d" % i], 1)
        free.append(("co", 4))
        obank.append(base)
    acc = 512 * ROT
    early = NP - LATE
    tw("qU", 1)
    lbank = []
    for q in range(4):
        a = len(free)
        lbank.append((512 * (a % ROT), free[a - ROT]))
        free.append(None)
    for s in range(NP):
        sp, sm = _plan(topo, cores, peers[s])
        te.wait_ge(sem["arr%d" % s], 2 * len(_bits(sm[sp.index(core)])))
        if s < early:
            mm = te.matmul_mx(T.ps[:, acc:acc + TE], T.lq[:, TW * s:TW * (s + 1)], T.lsc[:, TW * s:TW * (s + 1)],
                              T.uq[:], T.usc[:], s == 0, s == early - 1)
            if s == early - 1:
                mm.then_inc(sem.dec, 1)
        else:
            for q in range(4):
                base, fr = lbank[q]
                tw(*fr)
                mm = te.matmul_mx(T.ps[:, base:base + TW], T.lq[:, TW * s:TW * (s + 1)], T.lsc[:, TW * s:TW * (s + 1)],
                                  T.uq[:, TW * q:TW * (q + 1)], T.usc[:, TW * q:TW * (q + 1)], s == early, s == NP - 1)
                if s == NP - 1:
                    mm.then_inc(sem["dl%d" % q], 1)

    for k in range(NP):
        sc.wait_ge(sem["ml%d" % k], 1)
        for i in (0, 1):
            sc.activation(T.h[:, TE * k + i:TE * (k + 1):4], T.ps[:, bank[(k, 0)] + TW * i:bank[(k, 0)] + TW * (i + 1)],
                          Copy).then_inc(sem["cl%d" % k], 1)
        sc.wait_ge(sem["mh%d" % k], 1)
        sc.activation(T.h[:, TE * k + 2:TE * (k + 1):4], T.ps[:, bank[(k, 1)]:bank[(k, 1)] + TW],
                      Copy).then_inc(sem["ch%d" % k], 1)
    for i in range(4):
        sc.wait_ge(sem["mo%d" % i], 1)
        sc.activation(T.own[:, i:TE:4], T.ps[:, obank[i]:obank[i] + TW], Copy).then_inc(sem.co, 1)

    def q_a(hf):
        ve.wait_ge(sem["ldA%d" % hf], 16)
        ve.quantize_mx(T.aq[:, 2 * TW * hf:2 * TW * (hf + 1)], T.asc[:, 2 * TW * hf:2 * TW * (hf + 1)],
                       T.abf[:, half * hf:half * (hf + 1)]).then_inc(sem["qA%d" % hf], 1)

    def q_b(u):
        runs, lu = qunits[u]
        ve.wait_ge(sem["ldB%d" % lu], 16 * len(lunits[lu]))
        for lo, hi in runs:
            ve.quantize_mx(T.bq[:, TW * lo:TW * hi], T.bsc[:, TW * lo:TW * hi],
                           T.bbf[:, TE * lo:TE * hi]).then_inc(sem["qB%d" % u], 1)

    def tile(k):
        ve.wait_ge(sem["mh%d" % k], 1)
        ve.wait_ge(sem["cl%d" % k], 2)
        ve.wait_ge(sem["ch%d" % k], 1)
        ve.tensor_copy(T.h[:, TE * k + 3:TE * (k + 1):4],
                       T.ps[:, bank[(k, 1)] + TW:bank[(k, 1)] + 2 * TW]).then_inc(sem["cv%d" % k], 1)
        ve.wait_ge(sem["cv%d" % k], 1)
        ve.quantize_mx(T.hq[:, TW * k:TW * (k + 1)], T.hsc[:, TW * k:TW * (k + 1)],
                       T.h[:, TE * k:TE * (k + 1)]).then_inc(sem["qz%d" % k], 1)

    q_a(0)
    q_b(0)
    q_a(1)
    q_b(1)
    q_b(2)
    tile(0)
    tile(1)
    q_b(3)
    tile(2)
    q_b(4)
    tile(3)
    tile(4)
    q_b(5)
    tile(5)
    tile(6)

    sent = 0
    for k in range(NP):
        g.wait_ge(sem["qz%d" % k], 1)
        rid, pid = topo.addr(peers[k], core)
        s = _order(topo, cores, peers[k]).index(core)
        g.remote_dma(T.lq[:, TW * s:TW * (s + 1)].bitcast(dt.uint8), T.hq[:, TW * k:TW * (k + 1)].bitcast(dt.uint8),
                     sem["arr%d" % s], sem.snt, pid, rid, masks[k])
        g.remote_dma(T.lsc[:, TW * s:TW * (s + 1)], T.hsc[:, TW * k:TW * (k + 1)],
                     sem["arr%d" % s], sem.snt, pid, rid, masks[k])
        sent += 2 * len(_bits(masks[k]))
    g.wait_ge(sem.snt, sent)

    ve.wait_ge(sem.co, 4)
    ve.wait_ge(sem.dec, 1)
    ve.tensor_tensor(T.own[:], T.ps[:, acc:acc + TE], T.own[:], AluOpType.add).then_inc(sem.pm, 1)
    ve.wait_ge(sem.pm, 1)
    for q in range(4):
        ve.wait_ge(sem["dl%d" % q], 1)
        ve.tensor_tensor(T.ysb[:, TW * q:TW * (q + 1)], T.ps[:, lbank[q][0]:lbank[q][0] + TW],
                         T.own[:, TW * q:TW * (q + 1)], AluOpType.add).then_inc(sem["y%d" % (q // 2)], 1)
    hw = TE // 2
    sy.wait_ge(sem.y0, 2)
    sy.dma_start(T.y[:, 0:hw], T.ysb[:, 0:hw]).then_inc(sem.st0, 16)
    sc.wait_ge(sem.y1, 2)
    sc.dma_start(T.y[:, hw:TE], T.ysb[:, hw:TE]).then_inc(sem.st1, 16)
    sy.wait_ge(sem.st0, 16)
    sc.wait_ge(sem.st1, 16)
